import numpy as np, ml_dtypes
CORES = [51,54,179,182]
N = 4
BF = ml_dtypes.bfloat16
W, L, CAP, EQ, CNT, RO = 2048, 256, 64, 14, 9, 4
TAU = [96, 700, 24, 2496]
WA = np.array([7, 113, 51, 229, 87, 19, 161, 203, 35, 149, 71, 247, 93, 181, 125, 11])
WB = np.array([1, 3, 2, 7, 5, 1, 6, 3, 7, 2, 5, 4, 1, 6, 3, 5])
KP = np.array([3, 18, 45, 71, 102, 125, 150, 187, 208, 233, 260, 291, 318, 345, 382, 407])
KZ = np.array([0, 0, 0, 0, 0, 0, 25, 0, 0, 0, 1, 0, 0, 0, 0, 0])
TOP = 130560
def home(k):
    return (k @ WB) & (N - 1)
def look(k, n):
    u = (k @ WA) & (W - 1)
    return ((u * (2 * n + 1) >> 5)[..., None] + KP * u[..., None]) & (W - 1)
def whole8(x):
    return np.minimum(np.rint(np.asarray(x, np.float32)), TOP).astype(BF).astype(np.float32)
def pool(rng, keys):
    keys = keys[np.any(keys > 0, axis=1)]; z = home(keys); out = []
    for r in range(N):
        a = np.nonzero(z == r)[0]
        if len(a) == 0: a = np.arange(len(keys))
        out.append(keys[np.resize(rng.permutation(a), 4)])
    return np.stack(out)
def bend(rng, k, c, flip):
    n = len(k); i = (np.arange(16) * (2 * rng.integers(0, 8, (n, 1)) + 1) + rng.integers(0, 16, (n, 1))) & 15
    new = 255 - k if flip else (k + rng.integers(1, 256, k.shape)) & 255
    return np.where(i < np.asarray(c)[:, None], new, k)
def cut(rng, a, ln):
    col = np.arange(16)[None, :]; ln = np.asarray(ln)[:, None]
    a = np.where(col == ln, 0, a)
    return np.where((col > ln) & (rng.random((len(a), 1)) < 0.6), 0, a)
def thin(rng, k):
    i = np.where(rng.random(k) < 0.5, 15, rng.integers(0, 16, k))
    x = np.where(rng.random(k) < 0.5, rng.choice(np.array([1, 255]), k), rng.integers(1, 256, k))
    return np.where(np.arange(16)[None, :] == i[:, None], x[:, None], 0)
def nought(cand):
    at = np.nonzero((((cand @ WA) & (W - 1)) == 0) & ((home(cand) & 1) == 1))[0]
    return cand[at[0]] if len(at) else KZ
def keys_plain(rng):
    return rng.integers(0, 256, (512, 16))
def name_plain(rng, shape):
    return rng.integers(1, 256, shape)
def vt_plain(rng, k):
    x = np.exp2(8 + 9 * rng.random((k, 1))) * (0.25 + 0.75 * rng.random((k, 16)))
    x = np.where(rng.random((k, 16)) < 0.15, np.exp2(8 * rng.random((k, 16))) - 1, x)
    return whole8(np.where(rng.random((k, 1)) < 0.25, TOP, x))
def vl_plain(rng, k):
    x = np.exp2(11 + 6 * rng.random((k, 1))) * (0.25 + 0.75 * rng.random((k, 16)))
    return whole8(np.where(rng.random((k, 16)) < 0.1, np.exp2(8 * rng.random((k, 16))) - 1, x))
def make(rng, keys, flip, vt, vl, name, fill, lens):
    P = np.stack([pool(rng, keys(rng)) for g in range(8)]); few = [name(rng, 24) for g in range(8)]
    F = np.zeros((N, 8, W, 16), np.int64); G = np.zeros((N, 8, W, 16), np.int64); V = np.zeros((N, 8, W, 16), np.float32)
    f = np.zeros((N, 8, L, 16), np.int64); v = np.zeros((N, 8, L, 16), np.float32); nm = np.zeros((N, 8, L, 16), np.int64)
    for r in range(N):
        for g in range(8):
            Q = P[g].reshape(-1, 16)
            F[r, g] = bend(rng, P[g, r][rng.integers(0, 4, W)], rng.integers(0, 18 - EQ, W), flip) * (rng.random((W, 1)) < fill[g])
            G[r, g] = bend(rng, Q[rng.integers(0, len(Q), W)], rng.integers(0, 3, W) * (rng.random(W) < 0.2), flip)
            G[r, g] *= (rng.random((W, 1)) >= 0.04)
            V[r, g] = vt(rng, W)
            k = np.where(rng.random((L, 1)) < 0.7, P[g, r][rng.integers(0, 4, L)], Q[rng.integers(0, len(Q), L)])
            f[r, g] = bend(rng, k, rng.integers(0, 3, L) * (rng.random(L) < 0.2), flip) * (rng.random((L, 1)) >= 0.05)
            v[r, g] = vl(rng, L)
            a = np.where(rng.random((L, 16)) < 0.5, few[g][rng.integers(0, 24, (L, 16))], name(rng, (L, 16)))
            nm[r, g] = cut(rng, a, rng.choice(np.array(lens), L))
    return P, F, G, V, f, v, nm
def pack(F, G, V, f, v, nm):
    on = np.any(F > 0, axis=3, keepdims=True); d = {}
    for k, a in (("rf", F), ("rg", np.where(on, G, 0)), ("rv", np.where(on, V, 0)), ("wf", f), ("wv", v), ("nm", nm)):
        a = np.ascontiguousarray(np.swapaxes(a, 2, 3).reshape(N, 128, -1))
        d[k] = a.astype(np.int32) if k == "nm" else a.astype(np.float32).astype(BF)
    return d
def setup_inputs(rng):
    m = make(rng, keys_plain, False, vt_plain, vl_plain, name_plain, rng.uniform(0.4, 0.6, 8), [0, 1, 1, 2, 2, 3, 4, 6, 9, 16])
    return pack(*m[1:])
def setup_inputs_spread(rng):
    def keys(rng): return np.exp2(8 * rng.random((512, 16))).astype(np.int64) - 1
    def vt(rng, k): return whole8(np.exp2(17 * rng.random((k, 1))) * np.exp2(-3 * rng.random((k, 16))) * (rng.random((k, 16)) > 0.0625))
    def vl(rng, k): return whole8(np.exp2(9 + 8 * rng.random((k, 1))) * np.exp2(-3 * rng.random((k, 16))))
    def name(rng, shape): return np.exp2(8 * rng.random(shape)).astype(np.int64)
    m = make(rng, keys, False, vt, vl, name, rng.permutation(np.linspace(0.1, 0.95, 8)), [0, 1, 2, 3, 5, 8, 12, 15, 16])
    return pack(*m[1:])
def setup_inputs_near(rng):
    def keys(rng):
        b = np.repeat(rng.integers(0, 256, (1, 16)), 512, axis=0); return bend(rng, b, rng.integers(0, 19 - EQ, 512), False)
    def vt(rng, k):
        o = np.argsort(rng.random((k, 16)), axis=1); c = CNT - rng.integers(0, 2, (k, 1)); tau = np.array(TAU)[rng.integers(0, RO, (k, 1))]
        low = np.where((o == c) | (rng.random((k, 16)) < 0.5), tau, 0)
        a = whole8(np.where(o < c, TOP * (0.5 + 0.5 * rng.random((k, 16))), low))
        return np.where(rng.random((k, 1)) < 0.3, a, vt_plain(rng, k))
    def vl(rng, k):
        a = whole8(TOP * (0.5 + 0.5 * rng.random((k, 16))))
        return np.where(rng.random((k, 1)) < 0.6, a, vl_plain(rng, k))
    m = make(rng, keys, False, vt, vl, name_plain, rng.uniform(0.3, 0.7, 8), [0, 1, 2, 3, 4, 5, 7, 16])
    return pack(*m[1:])
def setup_inputs_ends(rng):
    def keys(rng): return 255 * rng.integers(0, 2, (512, 16))
    def vt(rng, k):
        a = np.where(rng.random((k, 16)) < 0.75, TOP, 0); z = rng.random((k, 1)); one = np.arange(16)[None, :] == rng.integers(0, 16, (k, 1))
        a = np.where((z >= 0.6) & (z < 0.75) & (a == 0) & (rng.random((k, 16)) < 0.5), 1, a)
        a = np.where(z < 0.6, TOP, a); a = np.where((z >= 0.4) & (z < 0.6) & one, 130048, a)
        return np.where(z > 0.95, 0, a).astype(np.float32)
    def vl(rng, k):
        a = np.where(rng.random((k, 16)) < 0.8, TOP, 0); z = rng.random((k, 1))
        a = np.where((z >= 0.8) & (z < 0.95) & (a == 0), 1, a); a = np.where(z < 0.5, TOP, a)
        return np.where(z > 0.95, 0, a).astype(np.float32)
    def name(rng, shape): return rng.choice(np.array([255] * 8 + [254, 1]), shape)
    P, F, G, V, f, v, nm = make(rng, keys, True, vt, vl, name, rng.uniform(0.4, 0.6, 8), [0, 1, 1, 2, 3, 15, 16, 16])
    col = np.arange(16)
    for g in range(8):
        Q = P[g].reshape(-1, 16); H = look(Q[:, None, :], np.arange(1, 256)[None, :]); at = np.argwhere(H == W - 1)
        odd = np.nonzero(((Q @ WA) & 1) == 1)[0]
        for r in range(N):
            away = odd[(odd >> 2) != r]
            if len(away):
                for lane, ln in ((L - 2, 16), (L // 2, 2), (1, 1)):
                    x = Q[away[rng.integers(0, len(away))]]; n = int(rng.choice(np.array([1, 255]))); h = look(x[None, :], np.array([n]))[0]
                    j = int(rng.integers(0, 16)); a = np.full((16, 16), TOP); a[:, j] = 0; a[15, j] = 1; a[1:15, (j + 1) & 15] = 0
                    F[r, g, h] = x; G[r, g, h] = Q[rng.permutation(len(Q))[:16]]; V[r, g, h] = a
                    f[r, g, lane] = x; v[r, g, lane] = TOP; nm[r, g, lane] = np.where(col == 0, n, np.where(col < ln, 255, 0))
            if len(at) == 0: continue
            i, n, m = at[rng.integers(0, len(at))]; h = H[i, n]
            F[r, g, h] = Q[i]; G[r, g, h] = Q[rng.integers(0, len(Q), 16)]
            a = np.full((16, 16), TOP); a[:m, rng.integers(0, 16)] = 130048; V[r, g, h] = a
            for lane, ln in ((0, 2), (L // 2 + 1, 16), (L - 1, 16)):
                f[r, g, lane] = Q[i]; v[r, g, lane] = TOP; nm[r, g, lane] = np.where(col == 0, n + 1, np.where(col < ln, 255, 0))
    return pack(F, G, V, f, v, nm)
def setup_inputs_corners(rng):
    fill = np.array([1.0, 0.0, 0.0, 0.0, 0.5, 0.5, 0.5, 0.5])
    P, F, G, V, f, v, nm = make(rng, keys_plain, False, vt_plain, vl_plain, name_plain, fill, [0, 1, 1, 2, 3, 15, 16])
    F[:, 0, :, 0] = np.maximum(F[:, 0, :, 0], 1)
    cand = rng.integers(0, 256, (131072, 16)); cand[:, 0] = np.maximum(cand[:, 0], 1)
    kz = nought(cand)
    H = look(cand, np.zeros(len(cand), np.int64)); at = np.argwhere(H == W - 1)
    for r in range(N):
        v[r, 0, ::2] = np.where(rng.random((L // 2, 1)) < 0.5, 0, TOP)
        for g in (1, 2, 3): nm[r, g] = cut(rng, rng.integers(1, 256, (L, 16)), rng.choice(np.array([1, 16]), L))
        f[r, 2] = P[2, (r + 1) % N][rng.integers(0, 4, L)]
        to = np.concatenate([np.full(CAP, (r + 1) % N), np.full(CAP + 1, (r + 2) % N), np.full(CAP - 1, (r + 3) % N), (r + np.arange(4, N)) % N]).astype(np.int64)
        f[r, 3] = 0; f[r, 3, rng.permutation(L)[:len(to)]] = P[3][to, rng.integers(0, 4, len(to))]
        f[r, 4] = 0
        if r % 2:
            for lane in (0, L // 2, L - 1): f[r, 4, lane] = P[4, r, lane % 4]
        f[r, 5] = P[5, r, 0]; nm[r, 5] = 0
        if r == N - 1: f[r, 5, 1::2] = P[5, r, 1]
        f[r, 6, 1::2] = kz; nm[r, 6] = cut(rng, rng.integers(1, 256, (L, 16)), np.where(np.arange(L) % 4 == 3, 16, rng.choice(np.array([1, 2, 16]), L)))
        F[r, 6, 0] = 0 if r % 2 else kz; G[r, 6, 0] = kz; V[r, 6, 0] = TOP; v[r, 6, 3::4] = TOP
        if len(at):
            i = at[rng.integers(0, len(at)), 0]; h = H[i]
            F[r, 7, h] = P[7, r][rng.integers(0, 4, 16)]; F[r, 7, h, 0] = np.maximum(F[r, 7, h, 0], 1); F[r, 7, W - 1] = 0
            for lane in ((L - 1,) if r % 2 else (5, L - 1)): f[r, 7, lane] = cand[i]; nm[r, 7, lane] = 0
    return pack(F, G, V, f, v, nm)
def setup_inputs_thin(rng):
    P, F, G, V, f, v, nm = make(rng, keys_plain, False, vt_plain, vl_plain, name_plain, rng.uniform(0.4, 0.6, 8), [0, 1, 1, 2, 2, 3, 4, 6, 9, 16])
    cand = rng.integers(0, 256, (131072, 16)); cand[:, 0] = np.maximum(cand[:, 0], 1)
    kz = nought(cand); z = int(home(kz))
    for r in range(N):
        f[r, 0] = rng.integers(0, 256, (L, 16)); nm[r, 0, :, 0] *= (rng.random(L) < 0.25 * (r & 1))
        F[r, 1] = thin(rng, W) * (rng.random((W, 1)) < 0.5); G[r, 1] = np.where(rng.random((W, 1)) < 0.5, thin(rng, W), G[r, 1])
        f[r, 1] = thin(rng, L); nm[r, 1, ::2, 0] = 0
        for g in (2, 3):
            G[r, g] *= (rng.random((W, 1)) >= 0.5); V[r, g] = np.where(rng.random((W, 1)) < 0.5, TOP, V[r, g])
            v[r, g] = np.where(rng.random((L, 1)) < 0.5, TOP, v[r, g])
            nm[r, g] = cut(rng, rng.integers(1, 256, (L, 16)), rng.choice(np.array([2, 3, 4, 16]), L))
        keep = rng.permutation(L)[:CAP // 2]; m = np.zeros((L, 1), np.int64); m[keep] = 1
        f[r, 6] *= m; nm[r, 6, :, 0] = np.maximum(nm[r, 6, :, 0], 1)
        F[r, 6, 0] = 0 if r == z else kz; G[r, 6, 0] = P[6, (r + 1) % N, 0]; V[r, 6, 0] = TOP
        if r == 0: f[r, 6] = 0
        elif r != z:
            f[r, 6, keep[:3]] = kz; v[r, 6, keep[:3]] = TOP; nm[r, 6, keep[:3]] = cut(rng, rng.integers(1, 256, (3, 16)), np.ones(3, np.int64))
    F[0, 2, 0] = np.where(rng.permutation(16) < 16 - EQ, rng.integers(1, 256, 16), 0); F[0, 3, 0] = thin(rng, 1)[0]
    for g in (2, 3): G[0, g, 0] = P[g, N - 1, 0]; V[0, g, 0] = TOP
    return pack(F, G, V, f, v, nm)
def check_inputs(d):
    bad = []
    for k, hi in (("rf", 255), ("rg", 255), ("rv", TOP), ("wf", 255), ("wv", TOP), ("nm", 255)):
        a = np.asarray(d[k]).astype(np.float64)
        if not np.all((a >= 0) & (a <= hi) & (a == np.floor(a))): bad.append("range of " + k)
    on = np.any(np.asarray(d["rf"]).astype(np.float32).reshape(N, 8, 16, W) != 0, axis=2, keepdims=True)
    for k in ("rg", "rv"):
        if np.any((np.asarray(d[k]).astype(np.float32).reshape(N, 8, 16, W) != 0) & ~on): bad.append("empty places of " + k)
    return bad
def reference(rf, rg, rv, wf, wv, nm):
    F, G, V = [a.astype(np.float32).astype(np.int32).reshape(N, 8, 16, W) for a in (rf, rg, rv)]
    f, v = [a.astype(np.float32).astype(np.int64).reshape(N, 8, 16, L) for a in (wf, wv)]
    na = nm.astype(np.int64).reshape(N, 8, 16, L); f0 = f.copy(); n0 = na[:, :, 0].copy()
    for t in range(RO):
        there = np.any(f0 != 0, axis=2)
        done = there & (na[:, :, 0] == 0); wait = there & (na[:, :, 0] != 0)
        q = np.where(done[:, :, None], f0, f); n = np.where(done, n0, na[:, :, 0])
        u = np.sum(WA[:, None] * q, axis=2) & (W - 1)
        h = ((u * (2 * n + 1) >> 5)[:, :, None] + KP[:, None] * u[:, :, None]) & (W - 1)
        ix = h.reshape(N, 8, 1, 16 * L)
        Fh = np.take_along_axis(F, ix, 3).reshape(N, 8, 16, 16, L)
        lo = np.minimum(np.take_along_axis(V, ix, 3).reshape(N, 8, 16, 16, L), v[:, :, :, None, :].astype(np.int32))
        same = np.sum(Fh == f[:, :, :, None, :].astype(np.int32), axis=2); over = np.sum(lo > TAU[t], axis=2)
        ok = (same >= EQ) & (over >= CNT) & wait[:, :, None]
        best = np.argmax(np.where(ok, np.sum(lo, axis=2), -1), axis=2)
        hit = np.any(ok, axis=2)[:, :, None]; bh = np.take_along_axis(h, best[:, :, None], 2)
        Gb = np.take_along_axis(G, bh, 3); Vb = np.take_along_axis(V, bh, 3)
        free = np.all(Fh == 0, axis=2); can = np.any(free, axis=2) & done
        place = np.take_along_axis(h, np.argmax(free, axis=2)[:, :, None], 2)[:, :, 0]
        for r in range(N):
            for g in range(8):
                lanes = np.nonzero(can[r, g])[0]; pl, first = np.unique(place[r, g, lanes], return_index=True); w = lanes[first]
                F[r, g][:, pl] = f0[r, g][:, w]; G[r, g][:, pl] = f[r, g][:, w]; V[r, g][:, pl] = v[r, g][:, w]
        f = np.where(hit, Gb, f); v = np.where(hit, np.minimum(v, Vb), v)
        na = np.where(hit, np.concatenate([na[:, :, 1:], np.zeros((N, 8, 1, L), np.int64)], axis=2), na)
        if t < RO - 1:
            goal = np.sum(WB[:, None] * np.where(na[:, :, :1] == 0, f0, f), axis=2) & (N - 1)
            S = np.concatenate([f0, f, v, na, n0[:, :, None]], axis=2); S2 = np.zeros_like(S)
            for q in range(N):
                for d in range(N):
                    go = (wait[q] & (goal[q] == d)).astype(np.int64); before = np.add.accumulate(go, axis=1) - go
                    gi, li = np.nonzero((go == 1) & (before < CAP))
                    S2[d, gi, :, q * CAP + before[gi, li]] = S[q, gi, :, li]
            f0, f, v, na, n0 = S2[:, :, :16], S2[:, :, 16:32], S2[:, :, 32:48], S2[:, :, 48:64], S2[:, :, 64]
    yf = np.where(wait[:, :, None], f, 0); yv = np.where(wait[:, :, None], v, 0)
    z = [np.sum(a.reshape(N, 128, 32, W // 32), axis=2).astype(np.float32) for a in (F, G, V)]
    return {"zf": z[0], "zg": z[1], "zv": z[2], "yf": yf.reshape(N, 128, L).astype(np.float32).astype(BF), "yv": yv.reshape(N, 128, L).astype(np.float32).astype(BF)}

from concourse.bass import DstId, RemoteDMATransfer
from concourse.mybir import AluOpType, AxisListType, ActivationFunctionType

W, L, RO = 2048, 256, 4
TAU = [96, 700, 24, 2496]
WA = [7, 113, 51, 229, 87, 19, 161, 203, 35, 149, 71, 247, 93, 181, 125, 11]
WB = [1, 3, 2, 7, 5, 1, 6, 3, 7, 2, 5, 4, 1, 6, 3, 5]
KP = [3, 18, 45, 71, 102, 125, 150, 187, 208, 233, 260, 291, 318, 345, 382, 407]
TOP = 130560
TOPC, ZV, DUMP, NEG = 2048, 2064, 2080, 2336
CS0 = 2336
LAND = [2592, 3616, 4640, 5664]
ZG = 6688
SB = 272
DK = [KP[m] - KP[m + 1] for m in range(15)]
DIAG = [1, -1, -2, 256, 4194304] + sorted(set(DK))
XN = ["a", "r0", "q", "qn", "r1", "one", "sev", "neg", "b", "big"]
MO = [sum(240 - 16 * k for k in range(c)) for c in range(16)]
BF, F4, I4, U2 = "bfloat16", "float32", "int32", "uint16"

SCRATCH = {}
for _n, _c, _d in [
    ("WF", NEG, BF), ("WG", ZG + 16, BF), ("WV", NEG, BF), ("IOT", NEG + 16, F4), ("NMI", 256, I4), ("NBM", 256, BF),
    ("AL", 256, BF), ("C1", 256, BF), ("FC", 256, BF), ("V4", 1024, BF), ("FG", 4096, BF), ("EQ", 4096, BF),
    ("LO", 4096, BF), ("GT", 4096, BF), ("PEN", 512, BF), ("MM", 256, F4), ("STP", 256, BF), ("ST", 4 * SB, BF),
    ("SD0", 1024, BF), ("SD1", 1024, BF), ("SD2", 1024, BF), ("ID0", 1280, BF), ("ID1", 1280, BF), ("ID2", 1280, BF),
    ("UI", 16, I4), ("UU", 16, I4), ("WW", 16, F4), ("YY", 16, I4), ("BS", 16, I4), ("H1", 256, F4), ("H2", 256, I4),
    ("H3", 256, I4), ("OFH", 256, U2), ("E1", 32, F4), ("WT", 16, F4), ("DR", 64, BF), ("GM", 80, F4), ("G1", 80, F4),
    ("G2", 80, F4), ("TA", 16, F4), ("TB", 16, I4), ("HB", 16, I4), ("OF", 80, F4), ("OFU", 80, U2), ("RI", 16, I4),
    ("CD", 16, I4), ("GO", 128, BF), ("SL", 64, F4), ("SLU", 16, U2), ("INV", 64, U2), ("PR", 256, F4),
    ("MA", 1920, BF), ("AB", 1920, BF), ("MD", 256, BF), ("CN", 256, BF), ("LA", 16, F4), ("LB", 16, F4), ("OFT", 16, U2),
    ("YF", 256, BF), ("YV", 256, BF), ("ZF", 64, F4), ("ZGS", 64, F4), ("ZVS", 64, F4),
    ("ZB", 256, BF), ("ON", 256, BF), ("IP", 16, I4), ("IQ", 16, I4), ("M16", 16, F4), ("AR", 16, F4), ("AC", 16, F4),
    ("M1", 128, BF), ("PF", 8, F4), ("BI", 8, BF), ("BI0", 8, BF), ("BL", 128, BF), ("BL0", 128, BF), ("BL4", 128, BF),
    ("U4", 128, BF), ("DG", 128 * len(DIAG), BF), ("XW", 144 * len(XN), BF), ("MT", 128, BF), ("SH", 128, BF),
    ("M2", 128, BF), ("LT", 128, BF), ("TR", 2048, BF), ("KF", 256, F4), ("RST", 256, F4), ("RS4", 64, F4),
    ("DC", 64, F4), ("SC", 64, BF), ("IDS", 256, BF), ("LW", 16, F4), ("DMP", 16, F4), ("DD", 320, F4), ("J1", 16, I4),
    ("J2", 16, I4), ("J3", 16, I4), ("J5", 8, I4), ("RH", 16, U2), ("IB", 16, U2), ("R5", 8, U2), ("BE", 16, F4)]:
    SCRATCH[_n] = ("sbuf", [128, _c], _d)
SCRATCH["PFC"] = ("psum", [128, 16, 4, 16], F4)
SCRATCH["PV4"] = ("psum", [128, 16, 4, 16], F4)
for _n in ("PK", "PN", "PA", "PB"):
    SCRATCH[_n] = ("psum", [128, 512], F4)
SEMAPHORES = ["qv", "qs", "qt", "qg", "sent", "arr1", "arr2", "arr3",
              "dwf", "dnm", "dwv", "drf", "drv", "drg", "dyf", "dyv", "dzf", "dzg", "dzv"]


def rank_program(g, core, T, topo):
    rank = T.rank_of(core)
    if rank is None:
        return
    A, AF = AluOpType, ActivationFunctionType
    NR = len(T.cores)
    Q = {"v": g.vector, "s": g.scalar, "t": g.tensor, "g": g, "y": g.sync}
    ops = []

    def V(n, *ix):
        shape = SCRATCH[n][1][1:]
        ix = list(ix) + [slice(None)] * (len(shape) - len(ix))
        lo = hi = 0
        for e, d in zip(ix, shape):
            if isinstance(e, slice):
                r = range(*e.indices(d))
                a, b = r[0], r[-1]
            else:
                a = b = e
            lo, hi = lo * d + a, hi * d + b
        if SCRATCH[n][0] == "psum":
            lo, hi = lo // 512 * 512, hi // 512 * 512 + 511
        return (T[n][tuple([slice(None)] + ix)], [(n, lo, hi + 1)])

    def S(n, a, b, s=1):
        return V(n, slice(a, b, s))

    def IND(w, o):
        return (w[0].indirect(o[0]), w[1], o[1])

    def ap(x):
        return x[0] if isinstance(x, tuple) else x

    def op(q, fn, outs, ins, sem=None, count=0):
        rd, wr = [], []
        for x in ins:
            if isinstance(x, tuple):
                rd += x[1] + (x[2] if len(x) > 2 else [])
        for x in outs:
            wr += x[1]
            rd += x[2] if len(x) > 2 else []
        ops.append({"q": q, "fn": fn, "rd": rd, "wr": wr, "sem": sem, "count": count})

    def tt(out, a, b, o):
        op("v", lambda: g.vector.tensor_tensor(out[0], a[0], b[0], o), [out], [a, b])

    def ts(out, a, s1, o1, s2=None, o2=None):
        if o2 is None:
            op("v", lambda: g.vector.tensor_scalar(out[0], a[0], ap(s1), None, o1), [out], [a, s1])
        else:
            op("v", lambda: g.vector.tensor_scalar(out[0], a[0], ap(s1), ap(s2), o1, o2), [out], [a, s1, s2])

    def cp(out, a):
        op("v", lambda: g.vector.tensor_copy(out[0], a[0]), [out], [a])

    def ms(out, c):
        op("v", lambda: g.vector.memset(out[0], c), [out], [])

    def red(out, a):
        op("v", lambda: g.vector.tensor_reduce(out[0], a[0], AxisListType.X, A.add), [out], [a])

    def scan(out, d0, d1, o0, o1):
        op("v", lambda: g.vector.tensor_tensor_scan(out[0], d0[0], d1[0], 0.0, o0, o1), [out], [d0, d1])

    def act(out, a, f=None, bias=0.0, scale=1.0):
        f = AF.Identity if f is None else f
        op("s", lambda: g.scalar.activation(out[0], a[0], f, bias=ap(bias), scale=ap(scale)), [out], [a, bias, scale])

    def mm(out, l, r, start, stop):
        op("t", lambda: g.tensor.matmul(out[0], l[0], r[0], start, stop), [out], [l, r])

    def iota(out, pat, base, ch=0):
        if SCRATCH[out[1][0][0]][2] == I4:
            op("g", lambda: g.iota(out[0], pat, base, ch), [out], [])
        else:
            op("g", lambda: g.iota(out[0], pat, base, ch, allow_small_or_imprecise_dtypes=True), [out], [])

    def aff(out, a, pat, cmp, fill, base, ch):
        op("g", lambda: g.affine_select(out[0], a[0], pat, cmp, float(fill), base, ch), [out], [a])

    def load(q, out, name):
        op(q, lambda: Q[q].dma_start(out[0], T[name][:]), [out], [], "d" + name, 16)

    def store(q, name, a):
        op(q, lambda: Q[q].dma_start(T[name][:], a[0]), [], [a], "d" + name, 16)

    def DGm(x):
        i = DIAG.index(x)
        return S("DG", 128 * i, 128 * i + 128)

    def X(n, r):
        o = 144 * XN.index(n) + 15 - r
        return S("XW", o, o + 128)

    def Xc(n, k=15):
        o = 144 * XN.index(n) + k
        return S("XW", o, o + 113, 16)

    def lane(t, a, r=0, s=1, e=256):
        if t == 0:
            o = LAND[0] + (0, 0, 256, 512)[a]
            return S("WG", o + r, o + e, s)
        return S("WG", LAND[t] + 4 * r + a, LAND[t] + 4 * e, 4 * s)

    def wrap(out, xn, src, start=True, stop=True):
        for r in range(16):
            mm(out, X(xn, r), src(r), start and r == 0, stop and r == 15)

    def diag(out, src, x, k=0):
        aff(out, src, [[-1, 128]], A.not_equal, x, k, 1)

    load("y", S("WG", LAND[0], LAND[0] + 256), "wf")
    load("s", V("NMI"), "nm")
    load("y", S("WG", LAND[0] + 256, LAND[0] + 512), "wv")
    load("s", S("WF", 0, W), "rf")
    load("y", S("WV", 0, W), "rv")
    load("y", S("WG", 0, W), "rg")

    Z128 = S("ZB", 0, 128)
    iota(V("IP"), [[-1, 16]], 128, 1)
    ms(V("ZB"), 0.0)
    ms(V("ON"), 1.0)
    ms(V("XW"), 0.0)
    for i in range(0, 16, 2):
        iota(S("AR", i, i + 2), [[WA[i + 1] - WA[i], 2]], WA[i])
    aff(V("BI0"), S("ON", 0, 8), [[-16, 8]], A.is_ge, 0, 0, 1)
    aff(V("BI"), V("BI0"), [[16, 8]], A.is_ge, 0, 15, -1)
    iota(V("J1"), [[0, 4], [4, 4]], 0)
    for m in range(16):
        act(S("KF", 64 * (m % 4) + m // 4, 64 * (m % 4) + 64, 4), S("ZB", 0, 16), bias=float(KP[m]))
    ts(V("IQ"), V("IP"), 15, A.bitwise_and)
    ts(V("M16"), V("IQ"), 0.0, A.is_equal)
    ts(S("J5", 0, 1), S("IQ", 0, 1), 2, A.logical_shift_right)
    tt(V("AC"), V("M16"), V("AR"), A.mult)
    ts(S("PF", 7, 8), S("M16", 0, 1), -1.0, A.mult)
    red(S("PF", 1, 2), S("M16", 0, 4))
    red(S("PF", 0, 1), V("AC"))
    cp(S("PF", 2, 3), S("J5", 0, 1))
    ts(Xc("a"), V("BI"), S("PF", 0, 1), A.mult)
    ts(Xc("r0"), V("BI"), S("M16", 0, 1), A.mult)
    ts(V("RH"), V("J1"), S("PF", 2, 3), A.add)
    ts(V("NBM"), V("NMI"), S("PF", 1, 2), A.mult)
    ts(S("PF", 5, 6), S("M16", 4, 5), 512.0, A.mult)
    diag(DGm(1), Z128, 1)
    aff(V("BL0"), S("ON", 0, 128), [[-16, 8], [0, 16]], A.is_ge, 0, 0, 1)
    aff(V("BL"), V("BL0"), [[16, 8], [0, 16]], A.is_ge, 0, 15, -1)
    for k in range(12, 16):
        act(Xc("qn", k), V("BI"), scale=S("PF", 7, 8))
    act(V("M1"), DGm(1), scale=512.0)
    act(DGm(-1), DGm(1), scale=-1.0)
    diag(V("M2"), V("M1"), 1, 4)
    act(V("MT"), V("BL"), scale=S("PF", 5, 6))
    diag(V("SH"), Z128, 1, -1)
    for x in DIAG[2:5]:
        diag(DGm(x), Z128, x)
    iota(V("J2"), [[16, 16]], 0)
    iota(V("J3"), [[1, 16]], 0)
    for t in range(RO):
        iota(S("DD", 80 * t + 16, 80 * t + 32), [[0, 16]], TOPC)
        iota(S("DD", 80 * t + 48, 80 * t + 64), [[0, 16]], NEG)
    iota(S("GM", 16, 32), [[0, 16]], 0)
    iota(V("RST"), [[0, 256]], 0)
    aff(S("RST", 0, 256, 16), S("RST", 0, 256, 16), [[0, 16]], A.is_gt, 1e12, 0, 0)
    iota(S("WV", TOPC, ZV), [[0, 16]], TOP)
    iota(S("WV", ZV, DUMP), [[0, 16]], 0)
    iota(S("WG", W, CS0), [[0, CS0 - W]], 0)
    iota(S("WG", LAND[0] + 768, LAND[1]), [[0, 256]], 0)
    iota(S("IOT", 0, NEG), [[1, NEG]], 0)
    iota(S("IOT", NEG, NEG + 16), [[0, 16]], -1)
    for i in range(16):
        aff(Xc("b"), Xc("b"), [[-16, 8]], A.not_equal, 2 * WB[i], -i, 1)
    iota(V("DC"), [[0, 16], [2, 4]], 1)
    iota(V("SC"), [[0, 16], [256, 4]], 4096)
    iota(V("RS4"), [[0, 64]], -1)
    iota(S("GO", 0, 64), [[0, 64]], 0)
    aff(V("LT"), V("BL"), [[1, 128]], A.is_gt, 0, 0, -1)
    diag(V("LT"), V("LT"), -4096)
    iota(V("IDS"), [[1, 256]], 0)

    def idfill(t):
        for d in range(NR):
            iota(S("ID%d" % t, 256 * d, 256 * d + 64), [[0, 64]], 256)

    def places(t):
        for b, o in ((0, 1), (32, 0), (64, 3)):
            act(S("DD", 80 * t + b, 80 * t + b + 16), V("LW"), bias=float(LAND[t] + o), scale=4.0)

    def consts_head():
        act(Xc("neg"), V("BI"), scale=-1.0)
        act(Xc("r1"), V("BI"), scale=S("M16", 1, 2))
        act(Xc("one"), V("BI"))
        act(Xc("sev"), V("BI"), scale=7.0)

    def consts_gap():
        cp(S("PF", 3, 4), S("IQ", 0, 1))
        ts(V("LW"), V("J2"), S("PF", 3, 4), A.add)
        cp(V("IB"), V("J3"))
        ts(V("R5"), S("ZB", 0, 8), S("PF", 3, 4), A.add)
        for b, o in ((0, 0), (32, 0), (64, 512)):
            ts(S("DD", b, b + 16), V("LW"), float(LAND[0] + o), A.add)
        ts(S("GM", 64, 80), V("LW"), float(CS0), A.add)
        for x in DIAG[5:]:
            ts(DGm(x), DGm(1), float(x), A.mult)

    def consts_choose():
        act(V("BL4"), V("BL"), scale=4096.0)
        act(V("TR"), S("EQ", 0, 2048), scale=0.0)
        act(S("RS4", 0, 64, 4), V("LW"), bias=1024.0)
        act(V("DMP"), V("LW"), bias=float(DUMP))
        act(S("PF", 6, 7), S("M16", 0, 1), scale=4096.0)
        act(Xc("big"), V("BI"), scale=S("PF", 6, 7))
        o = 144 * XN.index("q")
        act(S("XW", o, o + 144), S("XW", o + 144, o + 288), scale=-1.0)
        ts(S("J5", 2, 3), S("IQ", 0, 1), 3, A.bitwise_and)
        ts(S("PF", 4, 5), S("J5", 2, 3), float(SB), A.mult)
        aff(V("U4"), V("BL4"), [[1, 128]], A.is_gt, 0, 0, -1)
        for k in range(8):
            aff(S("TR", 16 * k, 2048, 129), S("U4", 16 * k, 16 * k + 16), [[0, 16]], A.is_ge, 0, 0, 0)

    idfill(0)
    for a in range(4):
        iota(S("ST", SB * a + 256, SB * a + SB), [[0, 16]], 0)
    iota(S("CN", 0, 16), [[0, 16]], 0)
    iota(S("WG", ZG, ZG + 16), [[0, 16]], 0)

    PU, PC1, PC0, PW0 = S("PA", 0, 16), S("PB", 0, 16), S("PB", 16, 32), S("PB", 32, 48)
    K256, N256, A256 = S("PK", 0, 256), S("PN", 0, 256), S("PA", 0, 256)

    def deal(q):
        can = {d: topo.engines(T.cores[q], T.cores[d]) for d in range(NR) if d != q}
        used, out = [], {}
        for d in sorted(can, key=lambda d: len(can[d])):
            free = [e for e in can[d] if e not in used]
            n = len(free) // len([c for c in can if c not in out and can[c] == can[d]])
            while 128 % n:
                n -= 1
            out[d] = free[:n]
            used += out[d]
        return out

    def arrive(t):
        op("x", None, [S("WG", LAND[t] + 256 * q, LAND[t] + 256 * q + 256) for q in range(NR) if q != rank], [],
           "arr%d" % t, sum(len(deal(q)[rank]) for q in range(NR) if q != rank))

    def send(t):
        tr, ins = [], []
        for d, es in deal(rank).items():
            rid, pid = topo.addr(T.cores[d], core)
            src = S("SD%d" % t, 256 * d, 256 * d + 256)
            o = LAND[t + 1] + 256 * rank
            ins.append(src)
            tr.append(RemoteDMATransfer(dst_ids=[DstId(rid=rid, pnc=pid)], dma_engine_mask=sum(1 << e for e in es),
                                        remote_sem=T.sem["arr%d" % (t + 1)], src=src[0], dst=T["WG"][:, o:o + 256]))
        op("g", lambda: g.remote_dma_fused(tr, local_sem=T.sem.sent), [], ins, "sent",
           -sum(len(e) for e in deal(rank).values()))

    def names0():
        mm(N256, V("BL"), lane(0, 1), True, True)
        mm(K256, V("M2"), V("NBM"), True, False)
        o = 144 * XN.index("qn") + 12
        mm(K256, S("XW", o, o + 128), V("NBM"), False, False)
        mm(K256, DGm(-1), V("ON"), False, True)
        act(V("AL"), N256, AF.Sign)

    def four(ps, src, hs=(0, 1)):
        for h in hs:
            for k in range(4):
                mm(V(ps, slice(8 * h, 8 * h + 8), k), DGm(1), src(128 * h, 128 * h + 128), True, True)

    def compare(t):
        mm(N256, DGm(1), lane(t, 1), True, False)
        mm(N256, V("MT"), lane(t, 3), False, True)
        act(V("FC"), N256, AF.Relu)

    def finished():
        ts(S("E1", 16, 32), PC0, 0.0, A.is_ge)

    def head(t):
        wrap(PU, "a", lambda r: lane(t, 1, r, 16))
        if t == 0:
            wrap(PW0, "r0", lambda r: S("NBM", r, 256, 16))
        else:
            wrap(PC0, "r0", lambda r: lane(t, 3, r, 16))
        four("PV4", lambda a, b: lane(t, 2, a, 1, b))
        cp(V("UI"), PU)
        act(V("WW"), PW0 if t == 0 else PC0, AF.Abs, bias=1.0, scale=2.0)
        ts(V("UU"), V("UI"), W - 1, A.bitwise_and)
        tt(V("H1"), IND(V("UU"), V("RH")), V("KF"), A.mult)
        tt(V("YY"), V("UU"), V("WW"), A.mult)
        act(S("V4", 0, 512), V("PV4", slice(0, 8)), AF.Copy)
        if t == 0:
            names0()
        else:
            finished()
            act(V("DR"), IND(S("E1", 16, 32), S("RH", 0, 4)), bias=1.0, scale=-1.0)
        act(S("V4", 512, 1024), V("PV4", slice(8, 16)), AF.Copy)
        if t > 0:
            compare(t)
        ts(V("BS"), V("YY"), 5, A.logical_shift_right)
        tt(V("H2"), IND(V("BS"), V("RH")), V("H1"), A.add)
        if t == 0:
            tt(V("C1"), V("NBM"), K256, A.min)
        ts(V("H3"), V("H2"), W - 1, A.bitwise_and)
        if t == 0:
            tt(lane(0, 3), V("C1"), V("AL"), A.mult)
            consts_head()
            compare(t)
            wrap(PC0, "r0", lambda r: lane(t, 3, r, 16))
        four("PFC", lambda a, b: S("FC", a, b))
        cp(V("OFH"), V("H3"))
        if t < RO - 1:
            if t > 0:
                wrap(PC1, "r1", lambda r: lane(t, 3, r, 16))
            mm(V("PV4", slice(0, 4)), V("SH"), lane(t, 3), True, True)

    def flags(t):
        d = 80 * t
        if t < RO - 1:
            ts(S("E1", 0, 16), PC1, 0.0, A.is_ge)
            ts(V("WT"), PC0, 0.0, A.is_gt)
            tt(S("GM", 32, 64), V("E1"), S("DD", d + 32, d + 64), A.mult)
            tt(S("GM", 0, 16), S("DD", d + 32, d + 48), S("GM", 32, 48), A.subtract)
        else:
            ts(S("GM", 0, 16), PC0, 0.0, A.is_le, float(ZG), A.mult)
            ts(S("GM", 16, 32), PC0, 0.0, A.is_le, float(ZV), A.mult)
            tt(S("GM", 48, 64), S("E1", 16, 32), S("DD", d + 48, d + 64), A.mult)

    def probes(t):
        def C(n, q, r=0, s=1):
            return S(n, 1024 * q + r, 1024 * q + 1024, s)

        def gv(q):
            tt(C("LO", q), IND(S("WV", 0, W), S("OFH", 64 * q, 64 * q + 64)), V("V4"), A.min)

        def gf(q):
            act(C("FG", q), IND(S("WF", 0, W), S("OFH", 64 * q, 64 * q + 64)), AF.Copy)

        def cnt(n, xn, q, ps, w):
            out = S(ps, q, 256, 4)
            if w:
                mm(out, DGm(w), V("DR"), True, False)
            wrap(out, xn, lambda r: C(n, q, r, 16), False, w != 0)

        def eq(q):
            tt(C("EQ", q), C("FG", q), V("PFC"), A.is_equal)

        def gt(q):
            act(C("GT", q), C("LO", q), AF.Sign, bias=-(TAU[t] + 0.5))

        mm(K256, DGm(1), V("ZB"), True, False)
        for q in range(4):
            gf(q); gv(q)
            if t == 0 and q == 0:
                finished()
                act(V("DR"), IND(S("E1", 16, 32), S("RH", 0, 4)), bias=1.0, scale=-1.0)
                wrap(PC1, "r1", lambda r: lane(t, 3, r, 16))
            cnt("LO", "neg", q, "PK", 0)
            gt(q); eq(q)
            cnt("GT", "sev", q, "PA", 256)
            if q == 3:
                if t < RO - 1:
                    act(S("WG", CS0, CS0 + 256), V("PV4", slice(0, 4)), AF.Copy)
                if t == 0:
                    consts_gap()
                act(S("PEN", 256, 512), A256, AF.Relu, bias=14.0, scale=-1.0)
            cnt("EQ", "one", q, "PN", -2)
        flags(t)
        if t > 0:
            write("WG", t - 1, 0)
        act(S("PEN", 0, 256), N256, AF.Relu, bias=14.0, scale=-1.0)
        mm(K256, DGm(4194304), S("PEN", 256, 512), False, False)
        mm(K256, DGm(4194304), S("PEN", 0, 256), False, True)

    def choose(t):
        d = 80 * t
        scan(V("MM"), V("RST"), K256, A.add, A.min)
        cp(V("BE"), S("MM", 15, 256, 16))
        tt(V("STP"), IND(V("BE"), V("IB")), V("MM"), A.is_equal)
        for m in range(15):
            mm(PU, DGm(DK[m]), S("STP", m, 256, 16), m == 0, m == 14)
        if t == 0:
            consts_choose()
        tt(V("G1"), IND(V("BE"), S("R5", 0, 5)), S("DD", d, d + 80), A.min)
        tt(V("G2"), V("G1"), V("GM"), A.max)
        tt(V("TA"), V("UU"), PU, A.mult)
        tt(V("TB"), V("TA"), S("H2", 195, 256, 4), A.add)
        ts(V("HB"), V("TB"), W - 1, A.bitwise_and)
        tt(V("OF"), IND(V("HB"), S("R5", 0, 5)), V("G2"), A.max)
        cp(V("OFU"), V("OF"))

    def pair_v(cs):
        for c in cs:
            ts(S("MA", MO[c], MO[c + 1]), S("PR", 16 * c + 16, 256), S("OF", 48 + c, 49 + c), A.is_equal)

    def pair_s(n):
        for c in range(n):
            act(S("AB", MO[c], MO[c + 1]), S("PR", 16 * c + 16, 256), AF.Abs, bias=S("OF", 48 + c, 49 + c), scale=-1.0)
        act(S("MA", 0, MO[n]), S("AB", 0, MO[n]), AF.Relu, bias=1.0, scale=-1.0)

    def pair_t(cs, first=False, final=False):
        if first:
            mm(K256, DGm(1), V("ZB"), True, False)
        for c in cs:
            mm(S("PK", 16 * c + 16, 256), V("BL"), S("MA", MO[c], MO[c + 1]), False, final and c == cs[-1])

    def pair_d():
        tt(V("MD"), IND(S("OF", 48, 64), V("IB")), V("PR"), A.is_equal)

    def pair_dt():
        for r in range(16):
            mm(S("PN", 0, 16), S("TR", 128 * r, 128 * r + 128), S("MD", r, 256, 16), r == 0, False)

    def winners():
        out = S("PN", 0, 16)
        act(S("CN", 16, 256), S("PK", 16, 256), AF.Copy)
        wrap(out, "big", lambda r: S("CN", r, 256, 16), False, True)
        tt(V("LA"), S("OF", 48, 64), out, A.add)
        tt(V("LB"), V("LA"), V("DMP"), A.min)
        cp(V("OFT"), V("LB"))

    def write(n, t, a):
        cp(IND(S(n, 0, NEG), V("OFT")), lane(t, a))

    def move(t):
        win = S("WG", 0, LAND[t] + 1024)
        cp(S("ST", SB, SB + 256), IND(win, S("OFU", 0, 16)))
        act(V("PR"), IND(V("IOT"), S("OFU", 48, 64)), AF.Copy)
        mm(PC1, DGm(1), S("ON", 0, 16), True, False)
        wrap(PC1, "b", lambda r: S("ST", SB + r, SB + 256, 16), False, True)
        tt(S("ST", 2 * SB, 2 * SB + 256), IND(S("WV", 0, DUMP), S("OFU", 16, 32)), lane(t, 2), A.min)
        act(S("ST", 0, 256), IND(win, S("OFU", 32, 48)), AF.Copy)
        act(S("ST", 3 * SB, 3 * SB + 256), IND(win, S("OFU", 64, 80)), AF.Copy)
        pair_v([14, 13])
        tt(V("RI"), V("WT"), PC1, A.mult)
        ts(V("CD"), V("RI"), 7, A.bitwise_and)
        tt(S("GO", 64, 128), IND(V("CD"), S("RH", 0, 4)), V("DC"), A.is_equal)
        P64 = S("PA", 0, 64)
        mm(P64, DGm(1), V("SC"), True, False)
        mm(P64, V("LT"), S("GO", 64, 128), False, False)
        for s in range(1, 16):
            mm(P64, V("BL"), S("GO", 64 - 4 * s, 128 - 4 * s), False, s == 15)
        pair_d()
        pair_v([12, 11])
        pair_s(6)
        scan(V("SL"), V("RS4"), P64, A.max, A.min)
        cp(V("SLU"), S("SL", 3, 64, 4))
        idw = "ID%d" % t
        cp(IND(V(idw), V("SLU")), V("IDS"))
        if t > 0:
            pair_dt()
        pair_t([14, 13, 12, 11], True)
        o = 144 * XN.index("q") + 12
        for dd in range(NR):
            for s in range(4):
                mm(S("PB", 16 * dd, 16 * dd + 16), S("XW", o - 4 * s, o - 4 * s + 128),
                   S(idw, 256 * dd + s, 256 * dd + 64, 4), s == 0, s == 3)
        if t == 0:
            pair_dt()
        pair_v([10, 9, 8, 7, 6])
        ts(V("INV"), S("PB", 0, 64), S("PF", 4, 5), A.add)
        far = [dd for dd in range(NR) if dd != rank]

        def take(dd, a, b):
            n, o = ("SD%d" % t, 256 * dd) if dd != rank else ("WG", LAND[t + 1] + 256 * rank)
            return S(n, o + 16 * a, o + 16 * b), IND(V("ST"), S("INV", 16 * dd + a, 16 * dd + b))

        cp(*take(far[0], 0, 16))
        act(*take(far[1], 0, 16), AF.Copy)
        cp(*take(far[2], 0, 8))
        act(*take(far[2], 8, 16), AF.Copy)
        send(t)
        pair_t([10, 9, 8, 7, 6, 0, 1, 2, 3, 4, 5], False, True)
        cp(*take(rank, 0, 16))
        winners()
        places(t + 1)
        if t < RO - 2:
            idfill(t + 1)

    def sums(n, ps, z, name, q):
        for k in range(32):
            mm(ps, DGm(1), S(n, 64 * k, 64 * k + 64), k == 0, k == 31)
        act(V(z), ps, AF.Copy)
        store(q, name, V(z))

    for t in range(RO):
        if t > 0:
            arrive(t)
        head(t)
        probes(t)
        choose(t)
        if t < RO - 1:
            move(t)
            write("WV", t, 2)
            write("WF", t, 1)
        else:
            act(V("PR"), IND(V("IOT"), S("OFU", 48, 64)), AF.Copy)
            tt(V("YV"), IND(S("WV", 0, DUMP), S("OFU", 16, 32)), lane(t, 2), A.min)
            store("y", "yv", V("YV"))
            pair_s(4)
            pair_d()
            pair_dt()
            pair_v(range(4, 15))
            pair_t(list(range(4, 15)) + [0, 1, 2, 3], True, True)
            cp(V("YF"), IND(V("WG"), S("OFU", 0, 16)))
            store("y", "yf", V("YF"))
            winners()
            write("WF", t, 1)
            sums("WF", S("PA", 0, 64), "ZF", "zf", "y")
            write("WV", t, 2)
            sums("WV", S("PB", 0, 64), "ZVS", "zv", "y")
            write("WG", t, 0)
            sums("WG", S("PK", 0, 64), "ZGS", "zg", "s")

    seen = {q: {} for q in Q}
    known, need, last = [], [], {}
    waited = set()
    for i, o in enumerate(ops):
        me = o["sem"] or o["q"]
        deps = set()
        for acc, mine in ((o["rd"], False), (o["wr"], True)):
            for n, lo, hi in acc:
                ps = SCRATCH[n][0] == "psum"
                for j, a, b, w in last.get(n, []):
                    if a < hi and lo < b:
                        same = (ops[j]["sem"] or ops[j]["q"]) == o["q"]
                        if (same and w and not mine) or (not same and (w or mine or ps)):
                            deps.add(j)
        for acc, mine in ((o["rd"], False), (o["wr"], True)):
            for n, lo, hi in acc:
                keep = [e for e in last.get(n, []) if not (
                    lo <= e[1] and e[2] <= hi and (mine or ((ops[e[0]]["sem"] or ops[e[0]]["q"]) == me and not e[3])))]
                last[n] = keep + [(i, lo, hi, mine)]
        mine = []
        kn = {}
        if o["q"] != "x":
            sq = seen[o["q"]]
            for j in sorted(deps, reverse=True):
                p = ops[j]["sem"] or ops[j]["q"]
                if sq.get(p, -1) < j:
                    mine.append(j)
                    waited.add(j)
                    for k, val in known[j].items():
                        sq[k] = max(sq.get(k, -1), val)
            kn = dict(sq)
        kn[me] = i
        known.append(kn)
        need.append(mine)
    total, value = {}, {}
    for i, o in enumerate(ops):
        if o["sem"] or i in waited:
            s = o["sem"] or "q" + o["q"]
            total[s] = total.get(s, 0) + (abs(o["count"]) or 1)
            value[i] = (s, total[s])
    top = {}
    for i, o in enumerate(ops):
        for j in need[i]:
            Q[o["q"]].wait_ge(T.sem[value[j][0]], value[j][1])
            top[value[j][0]] = max(top.get(value[j][0], 0), value[j][1])
        if o["fn"] is not None:
            ins = o["fn"]()
            if i in value and o["count"] >= 0:
                ins.then_inc(T.sem[value[i][0]], o["count"] or 1)
    for s in total:
        if top.get(s, 0) < total[s]:
            g.wait_ge(T.sem[s], total[s])
